import numpy as np, ml_dtypes
CORES = [127,119,111,103,95,87,79,71,63,55,47,39,31,23,15,7]
N = 16
def setup_inputs(rng):
    return {"x": rng.standard_normal((N, 128, 8), dtype=np.float32).astype(ml_dtypes.bfloat16)}
def reference(x):
    g = np.concatenate(list(x), axis=1)
    return {"y": np.broadcast_to(g, (N,) + g.shape)}

@@ -1,0 +1,54 @@
+from concourse.bass import DstId, RemoteDMATransfer
+
+W = 8
+HELPERS = 7
+
+SCRATCH = {
+    "xs": ("dram", [128, W], "bfloat16"),
+    "inbox": ("dram", [2, 128, W], "bfloat16"),
+    "land": ("sbuf", [128, 16 * W], "bfloat16"),
+}
+SEMAPHORES = ["loaded", "sent", "arr", "arrived", "stored"]
+
+
+def rank_program(g, core, T, topo):
+    k = core % 8
+    rank_core = core - k + 7
+    i = T.rank_of(rank_core)
+    if i is None:
+        return
+
+    def dst_id(c):
+        a = topo.addr(c)
+        return DstId(rid=a[0], pnc=a[1])
+
+    def cols(j):
+        return T.land[:, W * j:W * (j + 1)]
+
+    if k != 7:
+        h = k
+        g.wait_ge(T.sem.arr, 2)
+        g.remote_dma_fused(
+            [RemoteDMATransfer(dst_ids=[dst_id(rank_core)], dma_engine_mask=0xFF << (8 * s), remote_sem=T.sem.arrived,
+                               src=T.inbox[s], dst=cols(i ^ (2 * h + 2 + s)))
+             for s in (0, 1)],
+            local_sem=T.sem.sent)
+        g.wait_ge(T.sem.sent, 16)
+        return
+
+    g.sync.dma_start(T.xs[:], T.x[:]).then_inc(T.sem.loaded, 16)
+    g.scalar.dma_start(cols(i), T.x[:]).then_inc(T.sem.arrived, 16)
+    g.wait_ge(T.sem.loaded, 16)
+    transfers = []
+    for h in range(HELPERS):
+        ds = (2 * h + 3, 2 * h + 2)
+        transfers.append(RemoteDMATransfer(
+            dst_ids=[dst_id(T.cores[i ^ d] - 7 + h) for d in ds], dma_engine_mask=1 << h, remote_sem=T.sem.arr,
+            srcs=[T.xs[:]], dsts=[T.inbox[d & 1] for d in ds]))
+    g.remote_dma_fused(transfers, local_sem=T.sem.sent)
+    mate = topo.addr(T.cores[i ^ 1])
+    g.remote_dma(cols(i), T.xs[:], T.sem.arrived, T.sem.sent, mate[1], mate[0], 0x00FF)
+    g.sync.wait_ge(T.sem.arrived, 16 + 8 + HELPERS * 16)
+    g.sync.dma_start(T.y[:], T.land[:]).then_inc(T.sem.stored, 16)
+    g.sync.wait_ge(T.sem.stored, 16)
+    g.wait_ge(T.sem.sent, HELPERS + 8)

@@ -1,20 +1,17 @@
 from concourse.bass import DstId, RemoteDMATransfer
 
 W = 8
-HELPERS = 7
 
 SCRATCH = {
     "xs": ("dram", [128, W], "bfloat16"),
-    "inbox": ("dram", [2, 128, W], "bfloat16"),
-    "land": ("sbuf", [128, 16 * W], "bfloat16"),
+    "inbox": ("dram", [12, 128, W], "bfloat16"),
+    "quad": ("sbuf", [128, 4 * W], "bfloat16"),
 }
-SEMAPHORES = ["loaded", "sent", "arr", "arrived", "stored"]
+SEMAPHORES = ["loaded", "sent", "runs", "quadsem", "stored"]
 
 
 def rank_program(g, core, T, topo):
-    k = core % 8
-    rank_core = core - k + 7
-    i = T.rank_of(rank_core)
+    i = T.rank_of(core)
     if i is None:
         return
 
@@ -22,33 +19,30 @@ def rank_program(g, core, T, topo):
         a = topo.addr(c)
         return DstId(rid=a[0], pnc=a[1])
 
-    def cols(j):
-        return T.land[:, W * j:W * (j + 1)]
-
-    if k != 7:
-        h = k
-        g.wait_ge(T.sem.arr, 2)
-        g.remote_dma_fused(
-            [RemoteDMATransfer(dst_ids=[dst_id(rank_core)], dma_engine_mask=0xFF << (8 * s), remote_sem=T.sem.arrived,
-                               src=T.inbox[s], dst=cols(i ^ (2 * h + 2 + s)))
-             for s in (0, 1)],
-            local_sem=T.sem.sent)
-        g.wait_ge(T.sem.sent, 16)
-        return
-
+    mine = T.quad[:, W * (i & 3):W * ((i & 3) + 1)]
     g.sync.dma_start(T.xs[:], T.x[:]).then_inc(T.sem.loaded, 16)
-    g.scalar.dma_start(cols(i), T.x[:]).then_inc(T.sem.arrived, 16)
+    g.scalar.dma_start(mine, T.x[:]).then_inc(T.sem.quadsem, 16)
     g.wait_ge(T.sem.loaded, 16)
     transfers = []
-    for h in range(HELPERS):
-        ds = (2 * h + 3, 2 * h + 2)
+    for n in (0, 1):
+        ds = [4 + n + 2 * t for t in range(6)]
         transfers.append(RemoteDMATransfer(
-            dst_ids=[dst_id(T.cores[i ^ d] - 7 + h) for d in ds], dma_engine_mask=1 << h, remote_sem=T.sem.arr,
-            srcs=[T.xs[:]], dsts=[T.inbox[d & 1] for d in ds]))
+            dst_ids=[dst_id(T.cores[i ^ d]) for d in ds], dma_engine_mask=0x40 << n, remote_sem=T.sem.runs,
+            srcs=[T.xs[:]], dsts=[T.inbox[d - 4] for d in ds]))
+    for d in (1, 2, 3):
+        transfers.append(RemoteDMATransfer(
+            dst_ids=[dst_id(T.cores[i ^ d])], dma_engine_mask=0x3 << (2 * (d - 1)), remote_sem=T.sem.quadsem,
+            src=T.xs[:], dst=mine))
     g.remote_dma_fused(transfers, local_sem=T.sem.sent)
-    mate = topo.addr(T.cores[i ^ 1])
-    g.remote_dma(cols(i), T.xs[:], T.sem.arrived, T.sem.sent, mate[1], mate[0], 0x00FF)
-    g.sync.wait_ge(T.sem.arrived, 16 + 8 + HELPERS * 16)
-    g.sync.dma_start(T.y[:], T.land[:]).then_inc(T.sem.stored, 16)
-    g.sync.wait_ge(T.sem.stored, 16)
-    g.wait_ge(T.sem.sent, HELPERS + 8)
+
+    queues = (g.sync, g.scalar)
+    for q in queues:
+        q.wait_ge(T.sem.runs, 12)
+    for s in range(12):
+        j = i ^ (s + 4)
+        queues[s % 2].dma_start(T.y[:, W * j:W * (j + 1)], T.inbox[s]).then_inc(T.sem.stored, 16)
+    g.sync.wait_ge(T.sem.quadsem, 16 + 3 * 2)
+    b = 4 * W * (i // 4)
+    g.sync.dma_start(T.y[:, b:b + 4 * W], T.quad[:]).then_inc(T.sem.stored, 16)
+    g.wait_ge(T.sem.sent, 2 + 6)
+    g.wait_ge(T.sem.stored, 13 * 16)

from concourse.bass import DstId, RemoteDMATransfer

W = 8

SCRATCH = {
    "xs": ("dram", [128, W], "bfloat16"),
    "inbox": ("dram", [12, 128, W], "bfloat16"),
    "quad": ("sbuf", [128, 4 * W], "bfloat16"),
}
SEMAPHORES = ["loaded", "sent", "runs", "quadsem", "stored"]


def rank_program(g, core, T, topo):
    i = T.rank_of(core)
    if i is None:
        return

    def dst_id(c):
        a = topo.addr(c)
        return DstId(rid=a[0], pnc=a[1])

    mine = T.quad[:, W * (i & 3):W * ((i & 3) + 1)]
    g.sync.dma_start(T.xs[:], T.x[:]).then_inc(T.sem.loaded, 16)
    g.scalar.dma_start(mine, T.x[:]).then_inc(T.sem.quadsem, 16)
    g.wait_ge(T.sem.loaded, 16)
    transfers = []
    for n in (0, 1):
        ds = [4 + n + 2 * t for t in range(6)]
        transfers.append(RemoteDMATransfer(
            dst_ids=[dst_id(T.cores[i ^ d]) for d in ds], dma_engine_mask=0x40 << n, remote_sem=T.sem.runs,
            srcs=[T.xs[:]], dsts=[T.inbox[d - 4] for d in ds]))
    for d in (1, 2, 3):
        transfers.append(RemoteDMATransfer(
            dst_ids=[dst_id(T.cores[i ^ d])], dma_engine_mask=0x3 << (2 * (d - 1)), remote_sem=T.sem.quadsem,
            src=T.xs[:], dst=mine))
    g.remote_dma_fused(transfers, local_sem=T.sem.sent)

    queues = (g.sync, g.scalar)
    for q in queues:
        q.wait_ge(T.sem.runs, 12)
    for s in range(12):
        j = i ^ (s + 4)
        queues[s % 2].dma_start(T.y[:, W * j:W * (j + 1)], T.inbox[s]).then_inc(T.sem.stored, 16)
    g.sync.wait_ge(T.sem.quadsem, 16 + 3 * 2)
    b = 4 * W * (i // 4)
    g.sync.dma_start(T.y[:, b:b + 4 * W], T.quad[:]).then_inc(T.sem.stored, 16)
    g.wait_ge(T.sem.sent, 2 + 6)
    g.wait_ge(T.sem.stored, 13 * 16)
